import numpy as np
import ml_dtypes


def mxq(x, axis, fmt="e4m3"):
    dtype, down = {"e4m3": (ml_dtypes.float8_e4m3fn, 7), "e5m2": (ml_dtypes.float8_e5m2, 14)}[fmt]
    v = np.moveaxis(np.asarray(x, np.float32).astype(ml_dtypes.bfloat16).astype(np.float64), axis, -1)
    blocks = v.reshape(v.shape[:-1] + (-1, 32))
    amax = np.abs(blocks).max(-1, keepdims=True)
    byte = np.maximum(np.where(amax > 0, np.frexp(amax)[1] - 1 + 127, 0) - down, 1)
    scale = np.exp2(byte - 127.0)
    codes = (blocks / scale).astype(np.float32).astype(dtype).astype(np.float64)
    return np.moveaxis((codes * scale).reshape(v.shape), -1, axis)


WIDE = False


def mx_kscale(k):
    if not WIDE:
        return np.ones(k)
    levels = np.array([10, -10, 5, -5, 0])
    if k % 512:
        return np.exp2(np.random.permutation(np.resize(levels, k // 32))).repeat(32)
    a = np.empty((k // 512, 16))
    for p in range(k // 512):
        a[p, :8] = np.random.permutation(np.resize(levels, 8))
        for g in range(8):
            far = levels[np.abs(levels - a[p, g]) >= 10]
            a[p, g + 8] = far[np.random.randint(len(far))]
    return np.exp2(a.ravel()).repeat(32)


def f64(x):
    return np.asarray(x).astype(np.float64)


def striped(idx):
    return np.tile(np.asarray(idx).reshape(-1, 16).T, (8, 1)).astype(np.uint16)


def unstriped(offs):
    return offs[:16].T.reshape(-1).astype(np.int64)


E2M1 = np.array([0.0, 0.5, 1.0, 1.5, 2.0, 3.0, 4.0, 6.0, -0.0, -0.5, -1.0, -1.5, -2.0, -3.0, -4.0, -6.0])


def pack_weight(w, fmt):
    k, n = w.shape
    w = f64(np.asarray(w, np.float32).astype(ml_dtypes.bfloat16)).reshape(k // 32, 32, n)
    amax = np.abs(w).max(1)
    if fmt == "e4m3":
        byte = np.frexp(amax)[1] - 1 + 127 - 7
    else:
        mant, ex = np.frexp(amax / 6.0)
        byte = np.where(mant > 0.5, ex, ex - 1) + 127
    byte = np.clip(np.where(amax > 0, byte, 1), 1, 254)
    scaled = (w * np.exp2(127.0 - byte)[:, None, :]).reshape(k, n).astype(np.float32)
    by_word = np.ascontiguousarray(scaled.reshape(k // 512, 128, 4, n).transpose(0, 1, 3, 2))
    if fmt == "e4m3":
        words = by_word.astype(ml_dtypes.float8_e4m3fn).view(np.uint8)
    else:
        c = by_word.astype(ml_dtypes.float4_e2m1fn).view(np.uint8) & 0xF
        words = (c[..., 0::2] | (c[..., 1::2] << 4)).reshape(k // 512, 128, 2 * n)
    return np.ascontiguousarray(words), np.ascontiguousarray(byte.astype(np.uint8).reshape(k // 512, 16, n))


def unpack_weight(words, scales, fmt):
    g, _, n = scales.shape
    words = np.ascontiguousarray(words).reshape(g, 128, n, -1)
    if fmt == "e4m3":
        vals = words.view(ml_dtypes.float8_e4m3fn).astype(np.float64)
    else:
        nib = np.empty((g, 128, n, 4), np.uint8)
        nib[..., 0::2] = words & 0xF
        nib[..., 1::2] = words >> 4
        vals = E2M1[nib]
    vals = vals * np.repeat(np.exp2(scales.astype(np.float64) - 127.0), 8, axis=1)[..., None]
    return vals.transpose(0, 1, 3, 2).reshape(g * 512, n)


def bf(x):
    return np.asarray(x, np.float32).astype(ml_dtypes.bfloat16)


def planes(Y):
    r, m = Y.shape
    b = f64(bf(Y)).reshape(r // 32, 32, m)
    amax = np.abs(b).max(1)
    byte = np.clip(np.where(amax > 0, np.frexp(amax)[1] - 1 + 127 - 7, 1), 1, 254)
    codes = (b * np.exp2(127.0 - byte)[:, None, :]).reshape(r, m).astype(np.float32).astype(ml_dtypes.float8_e4m3fn).view(np.uint8)
    words = codes.reshape(r // 512, 128, 4, m).transpose(0, 1, 3, 2)
    return np.ascontiguousarray(words), np.ascontiguousarray(byte.astype(np.uint8).reshape(r // 512, 16, m))


D, T, I, Q, E = 512, 2048, 512, 256, 512


def setup_inputs():
    n = np.random.standard_normal
    idx = np.random.permutation(T)[:I]
    fd = mx_kscale(D)
    fi = mx_kscale(I)
    ti = np.ones(T)
    ti[idx] = fi
    keysp = pack_weight(n((D, T)) / fd[:, None], "e2m1")
    return {
        "dquery": (n((D, Q)) * 0.25 / np.sqrt(D) * fd[:, None]).astype(np.float32),
        "keys_words": keysp[0],
        "keys_scales": keysp[1],
        "olds": (0.3 * n((Q, T))).astype(np.float32),
        "keepf": (np.random.uniform(0.5, 1.0, (Q, 1))).astype(np.float32),
        "size": (np.random.uniform(0.5, 2.0, (1, I)) * fi).astype(np.float32),
        "vals": (n((E, T)) / ti).astype(np.float32),
        "offs": striped(idx),
    }


def reference(dquery, keys_words, keys_scales, olds, keepf, size, vals, offs):
    idx = unstriped(offs)
    keysu = unpack_weight(keys_words, keys_scales, "e2m1")
    dqueryq = mxq(f64(dquery), 0, "e4m3")
    keysidxg = keysu[:, idx]
    a = dqueryq.T @ keysidxg
    s = a + f64(olds)[:, idx] * f64(keepf)
    p = np.exp(s - np.max(s, axis=1, keepdims=True))
    w = p * f64(size) / np.sum(p, axis=1, keepdims=True)
    wt = w.T
    vt = f64(vals)[:, idx].T
    vtq = mxq(vt, 0, "e4m3")
    wtq = mxq(wt, 0, "e4m3")
    o = vtq.T @ wtq
    words, scales = planes(o)
    return o, words, scales

@@ -1,0 +1,194 @@
+from contextlib import ExitStack
+
+import concourse.mybir as mybir
+from concourse.masks import make_identity
+
+D, T, I, Q, E = 512, 2048, 512, 256, 512
+FLOPS = 2 * D * Q * I + 2 * I * E * Q
+
+F32 = mybir.dt.float32
+BF16 = mybir.dt.bfloat16
+I32 = mybir.dt.int32
+U32 = mybir.dt.uint32
+U16 = mybir.dt.uint16
+U8 = mybir.dt.uint8
+FP8X4 = mybir.dt.float8_e4m3fn_x4
+FP4X4 = mybir.dt.float4_e2m1fn_x4
+ALU = mybir.AluOpType
+ACT = mybir.ActivationFunctionType
+AX = mybir.AxisListType
+
+P = 128
+PACK = 4
+HALVES = Q // P
+
+
+def tile_attend_scorestep_pl_kernel(tc, dquery, keys_words, keys_scales, olds, keepf, size, vals, offs, out_0, out_1, out_2):
+    nc = tc.nc
+    with ExitStack() as ctx:
+        sb = ctx.enter_context(tc.tile_pool(name="sb", bufs=1))
+        ps = ctx.enter_context(tc.psum_pool(name="ps", bufs=1))
+
+        offsets = sb.tile([P, I // 16], U16, name="offsets")
+        nc.sync.dma_start(offsets[:], offs)
+
+        key_bytes = sb.tile([P, T], U8, name="key_bytes")
+        nc.vector.memset(key_bytes[:].bitcast(I32), 0)
+        for quad in range(4):
+            nc.scalar.dma_start(key_bytes[32 * quad : 32 * quad + 4, :].bitcast(I32), keys_scales[0, 4 * quad : 4 * quad + 4, :].bitcast(I32))
+
+        key_words = sb.tile([P, T], U16, name="key_words")
+        nc.sync.dma_start(key_words[:].bitcast(I32), keys_words[0].bitcast(I32))
+        dq_raw = sb.tile([P, PACK, Q], F32, name="dq_raw")
+        nc.sync.dma_start(dq_raw[:], dquery.rearrange("(p j) q -> p j q", j=PACK))
+        old_pool = []
+        for h in range(HALVES):
+            tile = sb.tile([P, T], F32, name=f"old_pool{h}")
+            nc.sync.dma_start(tile[:], olds[h * P : (h + 1) * P, :])
+            old_pool.append(tile)
+        val_pool = []
+        vals_dealt = vals.rearrange("(p t) c -> p t c", t=PACK)
+        for t in range(PACK):
+            tile = sb.tile([P, T], F32, name=f"val_pool{t}")
+            nc.sync.dma_start(tile[:], vals_dealt[:, t, :])
+            val_pool.append(tile)
+
+        keep = sb.tile([P, HALVES], F32, name="keep")
+        with nc.allow_non_contiguous_dma(reason="one value a query row"):
+            nc.gpsimd.dma_start(keep[:], keepf.rearrange("(h p) o -> p (h o)", p=P))
+        size4 = sb.tile([P, PACK], F32, name="size4")
+        nc.gpsimd.dma_start(size4[:], size.rearrange("o (p r) -> p (o r)", r=PACK))
+        ident = sb.tile([P, P], F32, name="ident")
+        make_identity(nc, ident[:])
+
+        size_rows = ps.tile([P, PACK, P], F32, name="size_rows")
+        for r in range(PACK):
+            nc.tensor.transpose(size_rows[:, r, :], size4[:, r : r + 1].to_broadcast([P, P]), ident[:])
+
+        got_bytes = sb.tile([P, I], U8, name="got_bytes", align_bytes=64)
+        nc.vector.tensor_copy(got_bytes[:], key_bytes[:].indirect(offsets[:]))
+        got_words = sb.tile([P, I], U16, name="got_words", align_bytes=64)
+        nc.vector.tensor_copy(got_words[:], key_words[:].indirect(offsets[:]))
+
+        dq_grouped = sb.tile([P, Q, PACK], BF16, name="dq_grouped", align_bytes=64)
+        nc.scalar.copy(
+            dq_grouped[:].rearrange("p (c i) j -> p c j i", i=4),
+            dq_raw[:].rearrange("p j (c i) -> p c j i", i=4),
+        )
+        dq_codes = sb.tile([P, Q], U32, name="dq_codes", align_bytes=64)
+        dq_scales = sb.tile([P, Q], U8, name="dq_scales", align_bytes=64)
+        nc.vector.quantize_mx(out=dq_codes[:].bitcast(FP8X4), scales=dq_scales[:], in_=dq_grouped[:].rearrange("p q j -> p (q j)"))
+
+        change = []
+        for h in range(HALVES):
+            bank = ps.tile([P, I], F32, name=f"change{h}")
+            cols = slice(h * P, (h + 1) * P)
+            nc.tensor.matmul_mx(
+                out=bank[:], lhsT=dq_codes[:, cols].bitcast(FP8X4), lhsT_scale=dq_scales[:, cols],
+                rhs=got_words[:].bitcast(FP4X4), rhs_scale=got_bytes[:], start=True, stop=True,
+            )
+            change.append(bank)
+
+        w_grouped = sb.tile([P, Q, PACK], BF16, name="w_grouped", align_bytes=64)
+        w_codes = sb.tile([P, Q], U32, name="w_codes", align_bytes=64)
+        w_scales = sb.tile([P, Q], U8, name="w_scales", align_bytes=64)
+        probs, sums = [], []
+
+        def turn(bank, rows, grouped):
+            words = rows.bitcast(F32)
+            for u in range(2):
+                nc.tensor.transpose(bank[:, u, :], words[:, u : I // 2 : 2], ident[:])
+            nc.scalar.copy(grouped.rearrange("p c j -> p (c j)").bitcast(F32).rearrange("p (c u) -> p c u", u=2), bank[:].rearrange("p u c -> p c u"))
+
+        def scores(h):
+            got = sb.tile([P, I], F32, name=f"old_got{h}")
+            nc.vector.tensor_copy(got[:], old_pool[h][:].indirect(offsets[:]))
+            s = sb.tile([P, I], F32, name=f"score{h}")
+            nc.vector.scalar_tensor_tensor(s[:], got[:], keep[:, h : h + 1], change[h][:], ALU.mult, ALU.add)
+            neg_max = sb.tile([P, 1], F32, name=f"neg_max{h}")
+            nc.vector.tensor_reduce(neg_max[:], s[:], AX.X, ALU.max, negate=True)
+            p = sb.tile([P, I], F32, name=f"prob{h}")
+            total = sb.tile([P, 1], F32, name=f"total{h}")
+            nc.scalar.activation(p[:], s[:], ACT.Exp, bias=neg_max[:], scale=1.0, accum_out=total[:])
+            probs.append(p)
+            sums.append(total)
+
+        def weights(h):
+            inv = sb.tile([P, 1], F32, name=f"inv{h}")
+            nc.vector.reciprocal(inv[:], sums[h][:])
+            w = sb.tile([P, I], BF16, name=f"weight{h}", align_bytes=64)
+            nc.vector.scalar_tensor_tensor(
+                w[:].rearrange("p (s r) -> p s r", r=PACK), probs[h][:].rearrange("p (s r) -> p s r", r=PACK),
+                inv[:], size_rows[:].rearrange("p r s -> p s r"), ALU.mult, ALU.mult,
+            )
+            bank = ps.tile([P, 2, P], F32, name="w_turned", tag="w_turned")
+            turn(bank, w[:], w_grouped[:, h * P : (h + 1) * P, :])
+
+        v_grouped, v_codes, v_scales = [], [], []
+
+        def gather_values(t):
+            got = sb.tile([P, I], BF16, name=f"val_got{t}", align_bytes=64)
+            nc.vector.tensor_copy(got[:], val_pool[t][:].indirect(offsets[:]))
+            bank = ps.tile([P, 2, P], F32, name=f"v_turned{t % 2}", tag=f"v_turned{t % 2}")
+            grouped = sb.tile([P, P, PACK], BF16, name=f"v_grouped{t}", align_bytes=64)
+            turn(bank, got[:], grouped[:])
+            v_grouped.append(grouped)
+
+        result = [ps.tile([P, PACK, P], F32, name=f"result{h}") for h in range(HALVES)]
+
+        def quantise_values(t):
+            codes = sb.tile([P, P], U32, name=f"v_codes{t}", align_bytes=64)
+            scales = sb.tile([P, P], U8, name=f"v_scales{t}", align_bytes=64)
+            nc.vector.quantize_mx(out=codes[:].bitcast(FP8X4), scales=scales[:], in_=v_grouped[t][:].rearrange("p c j -> p (c j)"))
+            v_codes.append(codes)
+            v_scales.append(scales)
+
+        def multiply(t):
+            for h in range(HALVES):
+                cols = slice(h * P, (h + 1) * P)
+                nc.tensor.matmul_mx(
+                    out=result[h][:, t, :], lhsT=v_codes[t][:].bitcast(FP8X4), lhsT_scale=v_scales[t][:],
+                    rhs=w_codes[:, cols].bitcast(FP8X4), rhs_scale=w_scales[:, cols], start=True, stop=True,
+                )
+
+        out_dealt = out_0.rearrange("(p t) q -> p t q", t=PACK)
+
+        def store_rows(first):
+            staged = sb.tile([P, 2, Q], F32, name=f"staged{first}")
+            for h in range(HALVES):
+                nc.scalar.copy(staged[:, :, h * P : (h + 1) * P], result[h][:, first : first + 2, :])
+            return staged
+
+        scores(0)
+        scores(1)
+        weights(0)
+        gather_values(0)
+        weights(1)
+        gather_values(1)
+        quantise_values(0)
+        nc.vector.quantize_mx(out=w_codes[:].bitcast(FP8X4), scales=w_scales[:], in_=w_grouped[:].rearrange("p q j -> p (q j)"))
+        multiply(0)
+        gather_values(2)
+        quantise_values(1)
+        multiply(1)
+        staged = store_rows(0)
+        nc.sync.dma_start(out_dealt[:, 0:2, :], staged[:])
+        gather_values(3)
+        quantise_values(2)
+        multiply(2)
+        quantise_values(3)
+        multiply(3)
+
+        o_grouped = [sb.tile([P, P, PACK], BF16, name=f"o_grouped{h}", align_bytes=64) for h in range(HALVES)]
+        nc.scalar.copy(o_grouped[0][:], result[0][:].rearrange("p t q -> p q t"))
+        nc.vector.tensor_copy(o_grouped[1][:], result[1][:].rearrange("p t q -> p q t"))
+        o_codes = sb.tile([P, Q], U32, name="o_codes", align_bytes=64)
+        o_scales = sb.tile([P, Q], U8, name="o_scales", align_bytes=64)
+        for h in range(HALVES):
+            cols = slice(h * P, (h + 1) * P)
+            nc.vector.quantize_mx(out=o_codes[:, cols].bitcast(FP8X4), scales=o_scales[:, cols], in_=o_grouped[h][:].rearrange("p c j -> p (c j)"))
+        staged = store_rows(2)
+        nc.scalar.dma_start(out_dealt[:, 2:4, :], staged[:])
+        nc.sync.dma_start(out_1[0].rearrange("p c r -> p (c r)").bitcast(I32), o_codes[:].bitcast(I32))
+        for quad in range(4):
+            nc.sync.dma_start(out_2[0, 4 * quad : 4 * quad + 4, :].bitcast(I32), o_scales[32 * quad : 32 * quad + 4, :].bitcast(I32))

@@ -33,65 +33,57 @@ def tile_attend_scorestep_pl_kernel(tc, dquery, keys_words, keys_scales, olds, k
         nc.sync.dma_start(offsets[:], offs)
 
         key_bytes = sb.tile([P, T], U8, name="key_bytes")
-        nc.vector.memset(key_bytes[:].bitcast(I32), 0)
-        for quad in range(4):
-            nc.scalar.dma_start(key_bytes[32 * quad : 32 * quad + 4, :].bitcast(I32), keys_scales[0, 4 * quad : 4 * quad + 4, :].bitcast(I32))
-
+        nc.gpsimd.memset(key_bytes[:].bitcast(I32), 0)
         key_words = sb.tile([P, T], U16, name="key_words")
         nc.sync.dma_start(key_words[:].bitcast(I32), keys_words[0].bitcast(I32))
-        dq_raw = sb.tile([P, PACK, Q], F32, name="dq_raw")
-        nc.sync.dma_start(dq_raw[:], dquery.rearrange("(p j) q -> p j q", j=PACK))
-        old_pool = []
-        for h in range(HALVES):
-            tile = sb.tile([P, T], F32, name=f"old_pool{h}")
-            nc.sync.dma_start(tile[:], olds[h * P : (h + 1) * P, :])
-            old_pool.append(tile)
+        for quad in range(4):
+            nc.sync.dma_start(key_bytes[32 * quad : 32 * quad + 4, :].bitcast(I32), keys_scales[0, 4 * quad : 4 * quad + 4, :].bitcast(I32))
+        dq_rows = dquery.rearrange("(p j) q -> p j q", j=PACK)
+        dq_raw = [sb.tile([P, PACK, P], F32, name=f"dq_raw{h}") for h in range(HALVES)]
+        old_pool = [sb.tile([P, T], F32, name=f"old_pool{h}", tag=f"old_pool{h}", align_bytes=64) for h in range(HALVES)]
+        nc.sync.dma_start(dq_raw[0][:], dq_rows[:, :, 0:P])
+        nc.sync.dma_start(old_pool[0][:], olds[0:P, :])
+        keep = sb.tile([P, HALVES], F32, name="keep")
+        with nc.allow_non_contiguous_dma(reason="one value a query row"):
+            nc.sync.dma_start(keep[:], keepf.rearrange("(h p) o -> p (h o)", p=P))
+        nc.sync.dma_start(dq_raw[1][:], dq_rows[:, :, P : 2 * P])
+        size4 = sb.tile([P, PACK], F32, name="size4")
+        nc.sync.dma_start(size4[:], size.rearrange("o (p r) -> p (o r)", r=PACK))
+        nc.sync.dma_start(old_pool[1][:], olds[P : 2 * P, :])
         val_pool = []
         vals_dealt = vals.rearrange("(p t) c -> p t c", t=PACK)
         for t in range(PACK):
-            tile = sb.tile([P, T], F32, name=f"val_pool{t}")
+            tile = sb.tile([P, T], F32, name=f"val_pool{t}", tag=f"val_pool{t}", align_bytes=64)
             nc.sync.dma_start(tile[:], vals_dealt[:, t, :])
             val_pool.append(tile)
 
-        keep = sb.tile([P, HALVES], F32, name="keep")
-        with nc.allow_non_contiguous_dma(reason="one value a query row"):
-            nc.gpsimd.dma_start(keep[:], keepf.rearrange("(h p) o -> p (h o)", p=P))
-        size4 = sb.tile([P, PACK], F32, name="size4")
-        nc.gpsimd.dma_start(size4[:], size.rearrange("o (p r) -> p (o r)", r=PACK))
         ident = sb.tile([P, P], F32, name="ident")
         make_identity(nc, ident[:])
-
-        size_rows = ps.tile([P, PACK, P], F32, name="size_rows")
-        for r in range(PACK):
-            nc.tensor.transpose(size_rows[:, r, :], size4[:, r : r + 1].to_broadcast([P, P]), ident[:])
 
         got_bytes = sb.tile([P, I], U8, name="got_bytes", align_bytes=64)
         nc.vector.tensor_copy(got_bytes[:], key_bytes[:].indirect(offsets[:]))
         got_words = sb.tile([P, I], U16, name="got_words", align_bytes=64)
         nc.vector.tensor_copy(got_words[:], key_words[:].indirect(offsets[:]))
 
-        dq_grouped = sb.tile([P, Q, PACK], BF16, name="dq_grouped", align_bytes=64)
-        nc.scalar.copy(
-            dq_grouped[:].rearrange("p (c i) j -> p c j i", i=4),
-            dq_raw[:].rearrange("p j (c i) -> p c j i", i=4),
-        )
-        dq_codes = sb.tile([P, Q], U32, name="dq_codes", align_bytes=64)
-        dq_scales = sb.tile([P, Q], U8, name="dq_scales", align_bytes=64)
-        nc.vector.quantize_mx(out=dq_codes[:].bitcast(FP8X4), scales=dq_scales[:], in_=dq_grouped[:].rearrange("p q j -> p (q j)"))
-
         change = []
-        for h in range(HALVES):
-            bank = ps.tile([P, I], F32, name=f"change{h}")
-            cols = slice(h * P, (h + 1) * P)
+
+        def changes(h):
+            grouped = sb.tile([P, P, PACK], BF16, name=f"dq_grouped{h}", align_bytes=64)
+            nc.scalar.copy(
+                grouped[:].rearrange("p (c i) j -> p c j i", i=4),
+                dq_raw[h][:].rearrange("p j (c i) -> p c j i", i=4),
+            )
+            codes, scales = quantise(grouped[:], f"dq{h}", f"dq{h}_codes")
+            bank = ps.tile([P, I], F32, name=f"change{h}", tag=f"change{h}")
             nc.tensor.matmul_mx(
-                out=bank[:], lhsT=dq_codes[:, cols].bitcast(FP8X4), lhsT_scale=dq_scales[:, cols],
+                out=bank[:], lhsT=codes[:].bitcast(FP8X4), lhsT_scale=scales[:],
                 rhs=got_words[:].bitcast(FP4X4), rhs_scale=got_bytes[:], start=True, stop=True,
             )
             change.append(bank)
 
-        w_grouped = sb.tile([P, Q, PACK], BF16, name="w_grouped", align_bytes=64)
-        w_codes = sb.tile([P, Q], U32, name="w_codes", align_bytes=64)
-        w_scales = sb.tile([P, Q], U8, name="w_scales", align_bytes=64)
+        early = sb.tile([P, Q + 2 * P, PACK], BF16, name="early", align_bytes=64)
+        late = [sb.tile([P, P, PACK], BF16, name=f"late{t}", align_bytes=64) for t in range(2)]
+        v_grouped = [early[:, Q : Q + P, :], early[:, Q + P : Q + 2 * P, :], late[0][:], late[1][:]]
         probs, sums = [], []
 
         def turn(bank, rows, grouped):
@@ -100,9 +92,15 @@ def tile_attend_scorestep_pl_kernel(tc, dquery, keys_words, keys_scales, olds, k
                 nc.tensor.transpose(bank[:, u, :], words[:, u : I // 2 : 2], ident[:])
             nc.scalar.copy(grouped.rearrange("p c j -> p (c j)").bitcast(F32).rearrange("p (c u) -> p c u", u=2), bank[:].rearrange("p u c -> p c u"))
 
-        def scores(h):
+        old_got = []
+
+        def gather_old(h):
             got = sb.tile([P, I], F32, name=f"old_got{h}")
             nc.vector.tensor_copy(got[:], old_pool[h][:].indirect(offsets[:]))
+            old_got.append(got)
+
+        def scores(h):
+            got = old_got[h]
             s = sb.tile([P, I], F32, name=f"score{h}")
             nc.vector.scalar_tensor_tensor(s[:], got[:], keep[:, h : h + 1], change[h][:], ALU.mult, ALU.add)
             neg_max = sb.tile([P, 1], F32, name=f"neg_max{h}")
@@ -113,6 +111,17 @@ def tile_attend_scorestep_pl_kernel(tc, dquery, keys_words, keys_scales, olds, k
             probs.append(p)
             sums.append(total)
 
+        def weights_on_scalar(h):
+            inv = sb.tile([P, 1], F32, name=f"inv{h}", tag="old_pool1", align_bytes=64)
+            nc.vector.reciprocal(inv[:], sums[h][:])
+            share = sb.tile([P, PACK, P], F32, name="share")
+            nc.scalar.activation(share[:].rearrange("p r s -> p s r"), probs[h][:].rearrange("p (s r) -> p s r", r=PACK), ACT.Copy, scale=inv[:])
+            bank = ps.tile([P, PACK, P], F32, name="share_turned")
+            for r in range(PACK):
+                nc.tensor.transpose(bank[:, r, :], share[:, r, :], ident[:])
+            for r in range(PACK):
+                nc.scalar.activation(early[:, h * P : (h + 1) * P, r], bank[:, r, :], ACT.Copy, scale=size4[:, r : r + 1])
+
         def weights(h):
             inv = sb.tile([P, 1], F32, name=f"inv{h}")
             nc.vector.reciprocal(inv[:], sums[h][:])
@@ -121,63 +130,69 @@ def tile_attend_scorestep_pl_kernel(tc, dquery, keys_words, keys_scales, olds, k
                 w[:].rearrange("p (s r) -> p s r", r=PACK), probs[h][:].rearrange("p (s r) -> p s r", r=PACK),
                 inv[:], size_rows[:].rearrange("p r s -> p s r"), ALU.mult, ALU.mult,
             )
-            bank = ps.tile([P, 2, P], F32, name="w_turned", tag="w_turned")
-            turn(bank, w[:], w_grouped[:, h * P : (h + 1) * P, :])
+            bank = ps.tile([P, 2, P], F32, name="w_turned", tag="change1")
+            turn(bank, w[:], early[:, h * P : (h + 1) * P, :])
 
-        v_grouped, v_codes, v_scales = [], [], []
 
         def gather_values(t):
             got = sb.tile([P, I], BF16, name=f"val_got{t}", align_bytes=64)
             nc.vector.tensor_copy(got[:], val_pool[t][:].indirect(offsets[:]))
             bank = ps.tile([P, 2, P], F32, name=f"v_turned{t % 2}", tag=f"v_turned{t % 2}")
-            grouped = sb.tile([P, P, PACK], BF16, name=f"v_grouped{t}", align_bytes=64)
-            turn(bank, got[:], grouped[:])
-            v_grouped.append(grouped)
+            turn(bank, got[:], v_grouped[t])
 
         result = [ps.tile([P, PACK, P], F32, name=f"result{h}") for h in range(HALVES)]
 
-        def quantise_values(t):
-            codes = sb.tile([P, P], U32, name=f"v_codes{t}", align_bytes=64)
-            scales = sb.tile([P, P], U8, name=f"v_scales{t}", align_bytes=64)
-            nc.vector.quantize_mx(out=codes[:].bitcast(FP8X4), scales=scales[:], in_=v_grouped[t][:].rearrange("p c j -> p (c j)"))
-            v_codes.append(codes)
-            v_scales.append(scales)
+        def quantise(grouped, name, tag):
+            width = grouped.shape[1]
+            codes = sb.tile([P, width], U32, name=f"{name}_codes", tag=tag, align_bytes=64)
+            scales = sb.tile([P, width], U8, name=f"{name}_scales", align_bytes=64)
+            nc.vector.quantize_mx(out=codes[:].bitcast(FP8X4), scales=scales[:], in_=grouped.rearrange("p c j -> p (c j)"))
+            return codes, scales
 
-        def multiply(t):
+        def multiply(t, v_codes, v_scales, w_codes, w_scales):
             for h in range(HALVES):
                 cols = slice(h * P, (h + 1) * P)
                 nc.tensor.matmul_mx(
-                    out=result[h][:, t, :], lhsT=v_codes[t][:].bitcast(FP8X4), lhsT_scale=v_scales[t][:],
+                    out=result[h][:, t, :], lhsT=v_codes.bitcast(FP8X4), lhsT_scale=v_scales,
                     rhs=w_codes[:, cols].bitcast(FP8X4), rhs_scale=w_scales[:, cols], start=True, stop=True,
                 )
 
         out_dealt = out_0.rearrange("(p t) q -> p t q", t=PACK)
 
-        def store_rows(first):
-            staged = sb.tile([P, 2, Q], F32, name=f"staged{first}")
+        def store_rows(first, count):
+            staged = sb.tile([P, count, Q], F32, name=f"staged{first}")
             for h in range(HALVES):
-                nc.scalar.copy(staged[:, :, h * P : (h + 1) * P], result[h][:, first : first + 2, :])
+                nc.scalar.copy(staged[:, :, h * P : (h + 1) * P], result[h][:, first : first + count, :])
             return staged
 
+        changes(0)
+        gather_old(0)
         scores(0)
+        changes(1)
+        size_rows = ps.tile([P, PACK, P], F32, name="size_rows", tag="change0")
+        for r in range(PACK):
+            nc.tensor.transpose(size_rows[:, r, :], size4[:, r : r + 1].to_broadcast([P, P]), ident[:])
+
+        gather_old(1)
+        weights_on_scalar(0)
         scores(1)
-        weights(0)
         gather_values(0)
         weights(1)
         gather_values(1)
-        quantise_values(0)
-        nc.vector.quantize_mx(out=w_codes[:].bitcast(FP8X4), scales=w_scales[:], in_=w_grouped[:].rearrange("p q j -> p (q j)"))
-        multiply(0)
         gather_values(2)
-        quantise_values(1)
-        multiply(1)
-        staged = store_rows(0)
+        codes, scales = quantise(early[:], "early", "val_pool2")
+        for t in range(2):
+            cols = slice(Q + t * P, Q + (t + 1) * P)
+            multiply(t, codes[:, cols], scales[:, cols], codes, scales)
+        staged = store_rows(0, 2)
         nc.sync.dma_start(out_dealt[:, 0:2, :], staged[:])
         gather_values(3)
-        quantise_values(2)
-        multiply(2)
-        quantise_values(3)
-        multiply(3)
+        v_codes, v_scales = quantise(late[0][:], "late0", "val_pool3")
+        multiply(2, v_codes[:], v_scales[:], codes, scales)
+        staged = store_rows(2, 1)
+        nc.sync.dma_start(out_dealt[:, 2:3, :], staged[:])
+        v_codes, v_scales = quantise(late[1][:], "late1", "late1_codes")
+        multiply(3, v_codes[:], v_scales[:], codes, scales)
 
         o_grouped = [sb.tile([P, P, PACK], BF16, name=f"o_grouped{h}", align_bytes=64) for h in range(HALVES)]
         nc.scalar.copy(o_grouped[0][:], result[0][:].rearrange("p t q -> p q t"))
@@ -187,8 +202,9 @@ def tile_attend_scorestep_pl_kernel(tc, dquery, keys_words, keys_scales, olds, k
         for h in range(HALVES):
             cols = slice(h * P, (h + 1) * P)
             nc.vector.quantize_mx(out=o_codes[:, cols].bitcast(FP8X4), scales=o_scales[:, cols], in_=o_grouped[h][:].rearrange("p c j -> p (c j)"))
-        staged = store_rows(2)
-        nc.scalar.dma_start(out_dealt[:, 2:4, :], staged[:])
+        staged = store_rows(3, 1)
+        nc.scalar.dma_start(out_dealt[:, 3:4, :], staged[:])
         nc.sync.dma_start(out_1[0].rearrange("p c r -> p (c r)").bitcast(I32), o_codes[:].bitcast(I32))
         for quad in range(4):
-            nc.sync.dma_start(out_2[0, 4 * quad : 4 * quad + 4, :].bitcast(I32), o_scales[32 * quad : 32 * quad + 4, :].bitcast(I32))
+            queue = nc.sync if quad < 2 else nc.scalar
+            queue.dma_start(out_2[0, 4 * quad : 4 * quad + 4, :].bitcast(I32), o_scales[32 * quad : 32 * quad + 4, :].bitcast(I32))

@@ -33,20 +33,19 @@ def tile_attend_scorestep_pl_kernel(tc, dquery, keys_words, keys_scales, olds, k
         nc.sync.dma_start(offsets[:], offs)
 
         key_bytes = sb.tile([P, T], U8, name="key_bytes")
-        nc.gpsimd.memset(key_bytes[:].bitcast(I32), 0)
+        nc.gpsimd.memset(key_bytes[:, 0 : T // 2].bitcast(I32), 0)
+        nc.vector.memset(key_bytes[:, T // 2 : T].bitcast(I32), 0)
         key_words = sb.tile([P, T], U16, name="key_words")
         nc.sync.dma_start(key_words[:].bitcast(I32), keys_words[0].bitcast(I32))
+        dq_raw = sb.tile([P, PACK, Q], F32, name="dq_raw")
+        nc.sync.dma_start(dq_raw[:], dquery.rearrange("(p j) q -> p j q", j=PACK))
         for quad in range(4):
             nc.sync.dma_start(key_bytes[32 * quad : 32 * quad + 4, :].bitcast(I32), keys_scales[0, 4 * quad : 4 * quad + 4, :].bitcast(I32))
-        dq_rows = dquery.rearrange("(p j) q -> p j q", j=PACK)
-        dq_raw = [sb.tile([P, PACK, P], F32, name=f"dq_raw{h}") for h in range(HALVES)]
         old_pool = [sb.tile([P, T], F32, name=f"old_pool{h}", tag=f"old_pool{h}", align_bytes=64) for h in range(HALVES)]
-        nc.sync.dma_start(dq_raw[0][:], dq_rows[:, :, 0:P])
         nc.sync.dma_start(old_pool[0][:], olds[0:P, :])
         keep = sb.tile([P, HALVES], F32, name="keep")
         with nc.allow_non_contiguous_dma(reason="one value a query row"):
             nc.sync.dma_start(keep[:], keepf.rearrange("(h p) o -> p (h o)", p=P))
-        nc.sync.dma_start(dq_raw[1][:], dq_rows[:, :, P : 2 * P])
         size4 = sb.tile([P, PACK], F32, name="size4")
         nc.sync.dma_start(size4[:], size.rearrange("o (p r) -> p (o r)", r=PACK))
         nc.sync.dma_start(old_pool[1][:], olds[P : 2 * P, :])
@@ -67,19 +66,21 @@ def tile_attend_scorestep_pl_kernel(tc, dquery, keys_words, keys_scales, olds, k
 
         change = []
 
-        def changes(h):
-            grouped = sb.tile([P, P, PACK], BF16, name=f"dq_grouped{h}", align_bytes=64)
+        def changes():
+            grouped = sb.tile([P, Q, PACK], BF16, name="dq_grouped", align_bytes=64)
             nc.scalar.copy(
                 grouped[:].rearrange("p (c i) j -> p c j i", i=4),
-                dq_raw[h][:].rearrange("p j (c i) -> p c j i", i=4),
+                dq_raw[:].rearrange("p j (c i) -> p c j i", i=4),
             )
-            codes, scales = quantise(grouped[:], f"dq{h}", f"dq{h}_codes")
-            bank = ps.tile([P, I], F32, name=f"change{h}", tag=f"change{h}")
-            nc.tensor.matmul_mx(
-                out=bank[:], lhsT=codes[:].bitcast(FP8X4), lhsT_scale=scales[:],
-                rhs=got_words[:].bitcast(FP4X4), rhs_scale=got_bytes[:], start=True, stop=True,
-            )
-            change.append(bank)
+            codes, scales = quantise(grouped[:], "dq", "dq_codes")
+            for h in range(HALVES):
+                cols = slice(h * P, (h + 1) * P)
+                bank = ps.tile([P, I], F32, name=f"change{h}", tag=f"change{h}")
+                nc.tensor.matmul_mx(
+                    out=bank[:], lhsT=codes[:, cols].bitcast(FP8X4), lhsT_scale=scales[:, cols],
+                    rhs=got_words[:].bitcast(FP4X4), rhs_scale=got_bytes[:], start=True, stop=True,
+                )
+                change.append(bank)
 
         early = sb.tile([P, Q + 2 * P, PACK], BF16, name="early", align_bytes=64)
         late = [sb.tile([P, P, PACK], BF16, name=f"late{t}", align_bytes=64) for t in range(2)]
@@ -165,10 +166,9 @@ def tile_attend_scorestep_pl_kernel(tc, dquery, keys_words, keys_scales, olds, k
                 nc.scalar.copy(staged[:, :, h * P : (h + 1) * P], result[h][:, first : first + count, :])
             return staged
 
-        changes(0)
+        changes()
         gather_old(0)
         scores(0)
-        changes(1)
         size_rows = ps.tile([P, PACK, P], F32, name="size_rows", tag="change0")
         for r in range(PACK):
             nc.tensor.transpose(size_rows[:, r, :], size4[:, r : r + 1].to_broadcast([P, P]), ident[:])

from contextlib import ExitStack

import concourse.mybir as mybir
from concourse.masks import make_identity

D, T, I, Q, E = 512, 2048, 512, 256, 512
FLOPS = 2 * D * Q * I + 2 * I * E * Q

F32 = mybir.dt.float32
BF16 = mybir.dt.bfloat16
I32 = mybir.dt.int32
U32 = mybir.dt.uint32
U16 = mybir.dt.uint16
U8 = mybir.dt.uint8
FP8X4 = mybir.dt.float8_e4m3fn_x4
FP4X4 = mybir.dt.float4_e2m1fn_x4
ALU = mybir.AluOpType
ACT = mybir.ActivationFunctionType
AX = mybir.AxisListType

P = 128
PACK = 4
HALVES = Q // P


def tile_attend_scorestep_pl_kernel(tc, dquery, keys_words, keys_scales, olds, keepf, size, vals, offs, out_0, out_1, out_2):
    nc = tc.nc
    with ExitStack() as ctx:
        sb = ctx.enter_context(tc.tile_pool(name="sb", bufs=1))
        ps = ctx.enter_context(tc.psum_pool(name="ps", bufs=1))

        offsets = sb.tile([P, I // 16], U16, name="offsets")
        nc.sync.dma_start(offsets[:], offs)

        key_bytes = sb.tile([P, T], U8, name="key_bytes")
        nc.gpsimd.memset(key_bytes[:, 0 : T // 2].bitcast(I32), 0)
        nc.vector.memset(key_bytes[:, T // 2 : T].bitcast(I32), 0)
        key_words = sb.tile([P, T], U16, name="key_words")
        nc.sync.dma_start(key_words[:].bitcast(I32), keys_words[0].bitcast(I32))
        dq_raw = sb.tile([P, PACK, Q], F32, name="dq_raw")
        nc.sync.dma_start(dq_raw[:], dquery.rearrange("(p j) q -> p j q", j=PACK))
        for quad in range(4):
            nc.sync.dma_start(key_bytes[32 * quad : 32 * quad + 4, :].bitcast(I32), keys_scales[0, 4 * quad : 4 * quad + 4, :].bitcast(I32))
        old_pool = [sb.tile([P, T], F32, name=f"old_pool{h}", tag=f"old_pool{h}", align_bytes=64) for h in range(HALVES)]
        nc.sync.dma_start(old_pool[0][:], olds[0:P, :])
        keep = sb.tile([P, HALVES], F32, name="keep")
        with nc.allow_non_contiguous_dma(reason="one value a query row"):
            nc.sync.dma_start(keep[:], keepf.rearrange("(h p) o -> p (h o)", p=P))
        size4 = sb.tile([P, PACK], F32, name="size4")
        nc.sync.dma_start(size4[:], size.rearrange("o (p r) -> p (o r)", r=PACK))
        nc.sync.dma_start(old_pool[1][:], olds[P : 2 * P, :])
        val_pool = []
        vals_dealt = vals.rearrange("(p t) c -> p t c", t=PACK)
        for t in range(PACK):
            tile = sb.tile([P, T], F32, name=f"val_pool{t}", tag=f"val_pool{t}", align_bytes=64)
            nc.sync.dma_start(tile[:], vals_dealt[:, t, :])
            val_pool.append(tile)

        ident = sb.tile([P, P], F32, name="ident")
        make_identity(nc, ident[:])

        got_bytes = sb.tile([P, I], U8, name="got_bytes", align_bytes=64)
        nc.vector.tensor_copy(got_bytes[:], key_bytes[:].indirect(offsets[:]))
        got_words = sb.tile([P, I], U16, name="got_words", align_bytes=64)
        nc.vector.tensor_copy(got_words[:], key_words[:].indirect(offsets[:]))

        change = []

        def changes():
            grouped = sb.tile([P, Q, PACK], BF16, name="dq_grouped", align_bytes=64)
            nc.scalar.copy(
                grouped[:].rearrange("p (c i) j -> p c j i", i=4),
                dq_raw[:].rearrange("p j (c i) -> p c j i", i=4),
            )
            codes, scales = quantise(grouped[:], "dq", "dq_codes")
            for h in range(HALVES):
                cols = slice(h * P, (h + 1) * P)
                bank = ps.tile([P, I], F32, name=f"change{h}", tag=f"change{h}")
                nc.tensor.matmul_mx(
                    out=bank[:], lhsT=codes[:, cols].bitcast(FP8X4), lhsT_scale=scales[:, cols],
                    rhs=got_words[:].bitcast(FP4X4), rhs_scale=got_bytes[:], start=True, stop=True,
                )
                change.append(bank)

        early = sb.tile([P, Q + 2 * P, PACK], BF16, name="early", align_bytes=64)
        late = [sb.tile([P, P, PACK], BF16, name=f"late{t}", align_bytes=64) for t in range(2)]
        v_grouped = [early[:, Q : Q + P, :], early[:, Q + P : Q + 2 * P, :], late[0][:], late[1][:]]
        probs, sums = [], []

        def turn(bank, rows, grouped):
            words = rows.bitcast(F32)
            for u in range(2):
                nc.tensor.transpose(bank[:, u, :], words[:, u : I // 2 : 2], ident[:])
            nc.scalar.copy(grouped.rearrange("p c j -> p (c j)").bitcast(F32).rearrange("p (c u) -> p c u", u=2), bank[:].rearrange("p u c -> p c u"))

        old_got = []

        def gather_old(h):
            got = sb.tile([P, I], F32, name=f"old_got{h}")
            nc.vector.tensor_copy(got[:], old_pool[h][:].indirect(offsets[:]))
            old_got.append(got)

        def scores(h):
            got = old_got[h]
            s = sb.tile([P, I], F32, name=f"score{h}")
            nc.vector.scalar_tensor_tensor(s[:], got[:], keep[:, h : h + 1], change[h][:], ALU.mult, ALU.add)
            neg_max = sb.tile([P, 1], F32, name=f"neg_max{h}")
            nc.vector.tensor_reduce(neg_max[:], s[:], AX.X, ALU.max, negate=True)
            p = sb.tile([P, I], F32, name=f"prob{h}")
            total = sb.tile([P, 1], F32, name=f"total{h}")
            nc.scalar.activation(p[:], s[:], ACT.Exp, bias=neg_max[:], scale=1.0, accum_out=total[:])
            probs.append(p)
            sums.append(total)

        def weights_on_scalar(h):
            inv = sb.tile([P, 1], F32, name=f"inv{h}", tag="old_pool1", align_bytes=64)
            nc.vector.reciprocal(inv[:], sums[h][:])
            share = sb.tile([P, PACK, P], F32, name="share")
            nc.scalar.activation(share[:].rearrange("p r s -> p s r"), probs[h][:].rearrange("p (s r) -> p s r", r=PACK), ACT.Copy, scale=inv[:])
            bank = ps.tile([P, PACK, P], F32, name="share_turned")
            for r in range(PACK):
                nc.tensor.transpose(bank[:, r, :], share[:, r, :], ident[:])
            for r in range(PACK):
                nc.scalar.activation(early[:, h * P : (h + 1) * P, r], bank[:, r, :], ACT.Copy, scale=size4[:, r : r + 1])

        def weights(h):
            inv = sb.tile([P, 1], F32, name=f"inv{h}")
            nc.vector.reciprocal(inv[:], sums[h][:])
            w = sb.tile([P, I], BF16, name=f"weight{h}", align_bytes=64)
            nc.vector.scalar_tensor_tensor(
                w[:].rearrange("p (s r) -> p s r", r=PACK), probs[h][:].rearrange("p (s r) -> p s r", r=PACK),
                inv[:], size_rows[:].rearrange("p r s -> p s r"), ALU.mult, ALU.mult,
            )
            bank = ps.tile([P, 2, P], F32, name="w_turned", tag="change1")
            turn(bank, w[:], early[:, h * P : (h + 1) * P, :])


        def gather_values(t):
            got = sb.tile([P, I], BF16, name=f"val_got{t}", align_bytes=64)
            nc.vector.tensor_copy(got[:], val_pool[t][:].indirect(offsets[:]))
            bank = ps.tile([P, 2, P], F32, name=f"v_turned{t % 2}", tag=f"v_turned{t % 2}")
            turn(bank, got[:], v_grouped[t])

        result = [ps.tile([P, PACK, P], F32, name=f"result{h}") for h in range(HALVES)]

        def quantise(grouped, name, tag):
            width = grouped.shape[1]
            codes = sb.tile([P, width], U32, name=f"{name}_codes", tag=tag, align_bytes=64)
            scales = sb.tile([P, width], U8, name=f"{name}_scales", align_bytes=64)
            nc.vector.quantize_mx(out=codes[:].bitcast(FP8X4), scales=scales[:], in_=grouped.rearrange("p c j -> p (c j)"))
            return codes, scales

        def multiply(t, v_codes, v_scales, w_codes, w_scales):
            for h in range(HALVES):
                cols = slice(h * P, (h + 1) * P)
                nc.tensor.matmul_mx(
                    out=result[h][:, t, :], lhsT=v_codes.bitcast(FP8X4), lhsT_scale=v_scales,
                    rhs=w_codes[:, cols].bitcast(FP8X4), rhs_scale=w_scales[:, cols], start=True, stop=True,
                )

        out_dealt = out_0.rearrange("(p t) q -> p t q", t=PACK)

        def store_rows(first, count):
            staged = sb.tile([P, count, Q], F32, name=f"staged{first}")
            for h in range(HALVES):
                nc.scalar.copy(staged[:, :, h * P : (h + 1) * P], result[h][:, first : first + count, :])
            return staged

        changes()
        gather_old(0)
        scores(0)
        size_rows = ps.tile([P, PACK, P], F32, name="size_rows", tag="change0")
        for r in range(PACK):
            nc.tensor.transpose(size_rows[:, r, :], size4[:, r : r + 1].to_broadcast([P, P]), ident[:])

        gather_old(1)
        weights_on_scalar(0)
        scores(1)
        gather_values(0)
        weights(1)
        gather_values(1)
        gather_values(2)
        codes, scales = quantise(early[:], "early", "val_pool2")
        for t in range(2):
            cols = slice(Q + t * P, Q + (t + 1) * P)
            multiply(t, codes[:, cols], scales[:, cols], codes, scales)
        staged = store_rows(0, 2)
        nc.sync.dma_start(out_dealt[:, 0:2, :], staged[:])
        gather_values(3)
        v_codes, v_scales = quantise(late[0][:], "late0", "val_pool3")
        multiply(2, v_codes[:], v_scales[:], codes, scales)
        staged = store_rows(2, 1)
        nc.sync.dma_start(out_dealt[:, 2:3, :], staged[:])
        v_codes, v_scales = quantise(late[1][:], "late1", "late1_codes")
        multiply(3, v_codes[:], v_scales[:], codes, scales)

        o_grouped = [sb.tile([P, P, PACK], BF16, name=f"o_grouped{h}", align_bytes=64) for h in range(HALVES)]
        nc.scalar.copy(o_grouped[0][:], result[0][:].rearrange("p t q -> p q t"))
        nc.vector.tensor_copy(o_grouped[1][:], result[1][:].rearrange("p t q -> p q t"))
        o_codes = sb.tile([P, Q], U32, name="o_codes", align_bytes=64)
        o_scales = sb.tile([P, Q], U8, name="o_scales", align_bytes=64)
        for h in range(HALVES):
            cols = slice(h * P, (h + 1) * P)
            nc.vector.quantize_mx(out=o_codes[:, cols].bitcast(FP8X4), scales=o_scales[:, cols], in_=o_grouped[h][:].rearrange("p c j -> p (c j)"))
        staged = store_rows(3, 1)
        nc.scalar.dma_start(out_dealt[:, 3:4, :], staged[:])
        nc.sync.dma_start(out_1[0].rearrange("p c r -> p (c r)").bitcast(I32), o_codes[:].bitcast(I32))
        for quad in range(4):
            queue = nc.sync if quad < 2 else nc.scalar
            queue.dma_start(out_2[0, 4 * quad : 4 * quad + 4, :].bitcast(I32), o_scales[32 * quad : 32 * quad + 4, :].bitcast(I32))
